import numpy as np
import ml_dtypes


def mxq(x, axis, fmt="e4m3"):
    dtype, down = {"e4m3": (ml_dtypes.float8_e4m3fn, 7), "e5m2": (ml_dtypes.float8_e5m2, 14)}[fmt]
    v = np.moveaxis(np.asarray(x, np.float32).astype(ml_dtypes.bfloat16).astype(np.float64), axis, -1)
    blocks = v.reshape(v.shape[:-1] + (-1, 32))
    amax = np.abs(blocks).max(-1, keepdims=True)
    byte = np.maximum(np.where(amax > 0, np.frexp(amax)[1] - 1 + 127, 0) - down, 1)
    scale = np.exp2(byte - 127.0)
    codes = (blocks / scale).astype(np.float32).astype(dtype).astype(np.float64)
    return np.moveaxis((codes * scale).reshape(v.shape), -1, axis)


WIDE = False


def mx_kscale(k):
    if not WIDE:
        return np.ones(k)
    levels = np.array([10, -10, 5, -5, 0])
    if k % 512:
        return np.exp2(np.random.permutation(np.resize(levels, k // 32))).repeat(32)
    a = np.empty((k // 512, 16))
    for p in range(k // 512):
        a[p, :8] = np.random.permutation(np.resize(levels, 8))
        for g in range(8):
            far = levels[np.abs(levels - a[p, g]) >= 10]
            a[p, g + 8] = far[np.random.randint(len(far))]
    return np.exp2(a.ravel()).repeat(32)


def f64(x):
    return np.asarray(x).astype(np.float64)


def striped(idx):
    return np.tile(idx.reshape(-1, 16).T, (8, 1)).astype(np.uint16)


def unstriped(offs):
    return offs[:16].T.reshape(-1).astype(np.int64)


def striped8(idx):
    return np.concatenate([x.reshape(-1, 16).T for x in idx]).astype(np.uint16)


def runs(offs, k):
    lists = np.stack([offs[16 * r : 16 * r + 16].T.reshape(-1) for r in range(8)]).astype(np.int64)
    return lists[np.arange(k) % 512 // 64]


def pack_weight(w):
    k, n = w.shape
    w = f64(np.asarray(w, np.float32).astype(ml_dtypes.bfloat16)).reshape(k // 32, 32, n)
    amax = np.abs(w).max(1)
    byte = np.clip(np.where(amax > 0, np.frexp(amax)[1] - 1 + 127 - 7, 1), 1, 254)
    scaled = (w * np.exp2(127.0 - byte)[:, None, :]).reshape(k, n).astype(np.float32)
    words = np.ascontiguousarray(scaled.reshape(k // 512, 128, 4, n).transpose(0, 1, 3, 2)).astype(ml_dtypes.float8_e4m3fn).view(np.uint8)
    return words, np.ascontiguousarray(byte.astype(np.uint8).reshape(k // 512, 16, n))


def unpack_weight(words, scales):
    g, p, n, _ = words.shape
    vals = np.ascontiguousarray(words).view(ml_dtypes.float8_e4m3fn).astype(np.float64) * np.repeat(np.exp2(scales.astype(np.float64) - 127.0), 8, axis=1)[..., None]
    return vals.transpose(0, 1, 3, 2).reshape(g * 512, n)


def sigmoid(v):
    return 1.0 / (1.0 + np.exp(-np.maximum(v, -700.0)))


K, T, S, G, H, C, W = 512, 1024, 256, 2048, 512, 512, 128


def setup_inputs():
    n = np.random.standard_normal
    s = mx_kscale(K)[:, None]
    packed_xT = pack_weight(n((K, T)) * s)
    packed_dT = pack_weight(n((K, G)) / s)
    perm = np.random.permutation(S)
    return {
        "x_words": packed_xT[0],
        "x_scales": packed_xT[1],
        "d_words": packed_dT[0],
        "d_scales": packed_dT[1],
        "sl": np.random.uniform(1.0, 2.0, (H, 1)).astype(np.float32),
        "th": (0.5 * n((H, 1))).astype(np.float32),
        "gs": (np.random.uniform(0.5, 1.5, (K, 1)) / s).astype(np.float32),
        "offs": striped(np.random.permutation(T)[:S]),
        "k1": striped8(np.random.randint(0, G, (8, H))),
        "n1": striped(np.random.permutation(S)),
        "n2": striped(np.random.permutation(S)),
        "cand": striped8(np.random.randint(0, T, (8, C))),
        "n3": striped(perm[:W]),
        "n4": striped(perm[W:]),
        "n5": striped(np.random.permutation(S)),
    }


def reference(x_words, x_scales, d_words, d_scales, sl, th, gs, offs, k1, n1, n2, cand, n3, n4, n5):
    x_cand = unpack_weight(x_words, x_scales)[np.arange(K)[:, None], runs(cand, K)]
    d_k1 = unpack_weight(d_words, d_scales)[np.arange(K)[:, None], runs(k1, K)]
    xq = unpack_weight(x_words, x_scales)[:, unstriped(offs)]
    h = 0.0625 * (d_k1.T @ xq)
    ds = np.zeros((H, S))
    ds[:, unstriped(n1)] = h
    sg = sigmoid(f64(sl) * (ds[:, unstriped(n2)] - f64(th)))
    z = f64(gs) * (h * sg)
    s = 0.0625 * ((x_cand.T @ mxq(z, 0, "e4m3")))
    pa = s[:, unstriped(n3)]
    pb = s[:, unstriped(n4)]
    rb = pa - pb
    ds2 = np.zeros((C, S))
    ds2[:, unstriped(n3)] = pb
    dt = ds2.copy()
    dt[:, unstriped(n4)] = rb
    return np.maximum(dt, 0.5 * dt[:, unstriped(n5)])

@@ -1,0 +1,217 @@
+from contextlib import ExitStack
+
+import concourse.mybir as mybir
+
+K, T, S, G, H, C, W = 512, 1024, 256, 2048, 512, 512, 128
+FLOPS = 2 * K * H * S + 2 * K * C * S
+
+F32 = mybir.dt.float32
+BF16 = mybir.dt.bfloat16
+I32 = mybir.dt.int32
+U32 = mybir.dt.uint32
+U16 = mybir.dt.uint16
+U8 = mybir.dt.uint8
+FP8X4 = mybir.dt.float8_e4m3fn_x4
+ACT = mybir.ActivationFunctionType
+ALU = mybir.AluOpType
+
+P = 128
+PACK = 4
+BLOCK_P = 8
+QUAD = 32
+PER_COL = 16
+HALF = S // 2
+SIXTEENTH = 0.0625
+DS_COLS = 352
+DT_COLS = 264
+LAST = 64
+
+
+def tile_picked_pqhcerlswapd_none_p_kernel(
+    tc, x_words, x_scales, d_words, d_scales, sl, th, gs, offs, k1, n1, n2, cand, n3, n4, n5, out
+):
+    nc = tc.nc
+    with ExitStack() as ctx:
+        lists = ctx.enter_context(tc.tile_pool(name="lists", bufs=1))
+        keep = ctx.enter_context(tc.tile_pool(name="keep", bufs=1))
+        psum = ctx.enter_context(tc.psum_pool(name="psum", bufs=1))
+
+        def load_list(name, src):
+            held = lists.tile(list(src.shape), U16, name=name)
+            nc.sync.dma_start(held[:], src)
+            return held
+
+        def entries(held, first, count):
+            return held[:, first // PER_COL : (first + count) // PER_COL]
+
+        def load_words(name, src, cols):
+            held = keep.tile([P, cols], U32, name=name)
+            nc.scalar.dma_start(held[:].bitcast(I32), src[0].rearrange("p n t -> p (n t)").bitcast(I32))
+            return held
+
+        def load_scale_rows(name, src, cols, clearing):
+            held = keep.tile([P, cols], U8, name=name, tag=name, align_bytes=64)
+            clearing.memset(held[:].bitcast(I32), 0)
+            nc.sync.dma_start(held[0:P:BLOCK_P, :].bitcast(I32), src[0].bitcast(I32))
+            return held
+
+        def load_rows(name, src):
+            held = keep.tile([P, PACK], F32, name=name)
+            nc.gpsimd.dma_start(held[:], src.rearrange("(p t) o -> p (t o)", t=PACK))
+            return held
+
+        def place_scale_rows(name, gathered, cols, queue):
+            plane = keep.tile([P, cols], U8, name=name, tag=name, align_bytes=64)
+            nc.vector.memset(plane[:].bitcast(I32), 0)
+            for q in range(0, P, QUAD):
+                queue.dma_start(plane[q : q + PACK, :].bitcast(I32), gathered[q : q + QUAD : BLOCK_P, :].bitcast(I32))
+            return plane
+
+        k1_l = load_list("k1_l", k1)
+        d_scale_tab = load_scale_rows("d_scale_tab", d_scales, G, nc.vector)
+        d_word_tab = load_words("d_word_tab", d_words, G)
+        offs_l = load_list("offs_l", offs)
+        x_scale_tab = load_scale_rows("x_scale_tab", x_scales, T, nc.vector)
+        x_word_tab = load_words("x_word_tab", x_words, T)
+        n1_l = load_list("n1_l", n1)
+        n2_l = load_list("n2_l", n2)
+        cand_l = load_list("cand_l", cand)
+        n3_l = load_list("n3_l", n3)
+        n4_l = load_list("n4_l", n4)
+        n5_l = load_list("n5_l", n5)
+        sl_t = load_rows("sl_t", sl)
+        th_t = load_rows("th_t", th)
+        gs_t = load_rows("gs_t", gs)
+
+        first_bytes = keep.tile([P, H + S], U8, name="first_bytes", tag="first_bytes", align_bytes=64)
+        nc.vector.tensor_copy(first_bytes[:, :H], d_scale_tab[:].indirect(k1_l[:]))
+        nc.vector.tensor_copy(first_bytes[:, H:], x_scale_tab[:].indirect(offs_l[:]))
+        first_plane = place_scale_rows("first_plane", first_bytes, H + S, nc.scalar)
+
+        d_picked = keep.tile([P, H], U32, name="d_picked", tag="d_scale_tab", align_bytes=64)
+        nc.vector.tensor_copy(d_picked[:], d_word_tab[:].indirect(k1_l[:]))
+        x_picked = keep.tile([P, S], U32, name="x_picked", align_bytes=64)
+
+        h, h_acc = [], []
+        for t in range(PACK):
+            d_dealt = keep.tile([P, P], U32, name=f"d_dealt{t}", align_bytes=64)
+            nc.vector.tensor_copy(d_dealt[:], d_picked[:, t:H:PACK])
+            if t == 0:
+                nc.vector.tensor_copy(x_picked[:], x_word_tab[:].indirect(offs_l[:]))
+            d_plane = keep.tile([P, P], U8, name=f"d_plane{t}", align_bytes=64)
+            nc.vector.tensor_copy(d_plane[:], first_plane[:, t:H:PACK])
+            acc = psum.tile([P, S], F32, name=f"h_acc{t}", tag=f"h_acc{t}")
+            nc.tensor.matmul_mx(
+                out=acc[:],
+                lhsT=d_dealt[:].bitcast(FP8X4),
+                lhsT_scale=d_plane[:],
+                rhs=x_picked[:].bitcast(FP8X4),
+                rhs_scale=first_plane[:, H:],
+                start=True,
+                stop=True,
+            )
+            h_t = keep.tile([P, S], F32, name=f"h{t}", tag=f"h{t}")
+            if t == 0:
+                nc.scalar.activation(h_t[:], acc[:], ACT.Copy, scale=SIXTEENTH)
+            else:
+                nc.vector.tensor_scalar(h_t[:], acc[:], SIXTEENTH, None, ALU.mult)
+            h.append(h_t)
+            h_acc.append(acc)
+
+        sl_th = keep.tile([P, PACK], F32, name="sl_th")
+        nc.gpsimd.tensor_tensor(sl_th[:], sl_t[:], th_t[:], ALU.mult)
+        bias = keep.tile([P, PACK], F32, name="bias")
+        nc.gpsimd.tensor_scalar(bias[:], sl_th[:], -1.0, 0.0, ALU.mult, ALU.add)
+
+        hg = keep.tile([P, PACK, S], F32, name="hg")
+        for t in range(PACK):
+            nc.vector.tensor_scalar(hg[:, t, :], h_acc[t][:], gs_t[:, t : t + 1], SIXTEENTH, ALU.mult, ALU.mult)
+
+        ds = []
+        for t in range(PACK):
+            ds_t = keep.tile([P, DS_COLS], F32, name=f"ds{t}")
+            nc.scalar.activation(ds_t[:].indirect(n1_l[:]), h[t][:], ACT.Copy)
+            ds.append(ds_t)
+
+        cand_bytes = keep.tile([P, C], U8, name="cand_bytes", tag="first_plane", align_bytes=64)
+        nc.vector.tensor_copy(cand_bytes[:], x_scale_tab[:].indirect(cand_l[:]))
+        cand_plane = place_scale_rows("cand_plane", cand_bytes, C, nc.sync)
+        cand_picked = keep.tile([P, C], U32, name="cand_picked", tag="first_bytes", align_bytes=64)
+        nc.vector.tensor_copy(cand_picked[:], x_word_tab[:].indirect(cand_l[:]))
+
+        tiles = C // P
+        s = [keep.tile([P, S], F32, name=f"s{u}") for u in range(tiles)]
+        sg = keep.tile([P, PACK, S], F32, name="sg", tag=f"h{PACK - 1}")
+        s_acc = {}
+        for j0 in range(0, S, HALF):
+            cols = slice(j0, j0 + HALF)
+            z_woven = keep.tile([P, HALF, PACK], BF16, name=f"z_woven{j0}", tag="z_woven", align_bytes=64)
+            for t in range(PACK):
+                nc.scalar.activation(
+                    sg[:, t, cols], ds[t][:].indirect(entries(n2_l, j0, HALF)), ACT.Sigmoid,
+                    bias=bias[:, t : t + 1], scale=sl_t[:, t : t + 1],
+                )
+                if t % 2 == 1:
+                    pair = slice(t - 1, t + 1)
+                    nc.vector.tensor_tensor(
+                        z_woven[:, :, pair],
+                        hg[:, pair, cols].rearrange("p t j -> p j t"),
+                        sg[:, pair, cols].rearrange("p t j -> p j t"),
+                        ALU.mult,
+                    )
+            z_words = keep.tile([P, HALF], U32, name=f"z_words{j0}", align_bytes=64)
+            z_plane = keep.tile([P, HALF], U8, name=f"z_plane{j0}", align_bytes=64)
+            nc.vector.quantize_mx(z_words[:].bitcast(FP8X4), z_plane[:], z_woven[:].rearrange("p j t -> p (j t)"))
+            for u in range(tiles):
+                rows = slice(u * P, (u + 1) * P)
+                s_acc[u, j0] = psum.tile([P, HALF], F32, name=f"s_acc{u}_{j0}", tag=f"s_acc{u}" if j0 == 0 else f"h_acc{u}")
+                nc.tensor.matmul_mx(
+                    out=s_acc[u, j0][:],
+                    lhsT=cand_picked[:, rows].bitcast(FP8X4),
+                    lhsT_scale=cand_plane[:, rows],
+                    rhs=z_words[:].bitcast(FP8X4),
+                    rhs_scale=z_plane[:],
+                    start=True,
+                    stop=True,
+                )
+        for u in range(tiles):
+            nc.scalar.activation(s[u][:, :HALF], s_acc[u, 0][:], ACT.Copy, scale=SIXTEENTH)
+        nc.scalar.activation(s[0][:, HALF:], s_acc[0, HALF][:], ACT.Copy, scale=SIXTEENTH)
+        for u in range(1, tiles):
+            nc.vector.tensor_scalar(s[u][:, HALF:], s_acc[u, HALF][:], SIXTEENTH, None, ALU.mult)
+
+        pb, rb, dt = {}, {}, {}
+
+        def fetch_pairs(u):
+            pa = keep.tile([P, W], F32, name=f"pa{u}")
+            pb[u] = keep.tile([P, W], F32, name=f"pb{u}")
+            rb[u] = keep.tile([P, W], F32, name=f"rb{u}")
+            nc.scalar.activation(pb[u][:], s[u][:].indirect(n4_l[:]), ACT.Copy)
+            nc.scalar.activation(pa[:], s[u][:].indirect(n3_l[:]), ACT.Copy)
+            nc.vector.tensor_tensor(rb[u][:], pa[:], pb[u][:], ALU.subtract)
+
+        def put_pb(u):
+            dt[u] = keep.tile([P, DT_COLS], F32, name=f"dt{u}")
+            nc.scalar.activation(dt[u][:].indirect(n3_l[:]), pb[u][:], ACT.Copy)
+
+        def put_rb(u):
+            nc.scalar.activation(dt[u][:].indirect(n4_l[:]), rb[u][:], ACT.Copy)
+
+        def finish(u, pieces):
+            for j0, width in pieces:
+                cols = slice(j0, j0 + width)
+                other = keep.tile([P, width], F32, name=f"other{u}_{j0}")
+                nc.scalar.activation(other[:], dt[u][:].indirect(entries(n5_l, j0, width)), ACT.Copy)
+                result = keep.tile([P, width], F32, name=f"result{u}_{j0}")
+                nc.vector.scalar_tensor_tensor(result[:], other[:], 0.5, dt[u][:, cols], ALU.mult, ALU.max)
+                nc.sync.dma_start(out[u * P : (u + 1) * P, cols], result[:])
+
+        for step in range(tiles + 3):
+            if step < tiles:
+                fetch_pairs(step)
+            if 2 <= step < tiles + 2:
+                put_rb(step - 2)
+            if 1 <= step < tiles + 1:
+                put_pb(step - 1)
+            if step >= 3:
+                finish(step - 3, [(0, S - LAST), (S - LAST, LAST)] if step - 3 == tiles - 1 else [(0, S)])

@@ -25,6 +25,7 @@ SIXTEENTH = 0.0625
 DS_COLS = 352
 DT_COLS = 264
 LAST = 64
+VECTOR_CLEARS = 3 * G // 4
 
 
 def tile_picked_pqhcerlswapd_none_p_kernel(
@@ -46,13 +47,7 @@ def tile_picked_pqhcerlswapd_none_p_kernel(
 
         def load_words(name, src, cols):
             held = keep.tile([P, cols], U32, name=name)
-            nc.scalar.dma_start(held[:].bitcast(I32), src[0].rearrange("p n t -> p (n t)").bitcast(I32))
-            return held
-
-        def load_scale_rows(name, src, cols, clearing):
-            held = keep.tile([P, cols], U8, name=name, tag=name, align_bytes=64)
-            clearing.memset(held[:].bitcast(I32), 0)
-            nc.sync.dma_start(held[0:P:BLOCK_P, :].bitcast(I32), src[0].bitcast(I32))
+            nc.sync.dma_start(held[:].bitcast(I32), src[0].rearrange("p n t -> p (n t)").bitcast(I32))
             return held
 
         def load_rows(name, src):
@@ -68,43 +63,50 @@ def tile_picked_pqhcerlswapd_none_p_kernel(
             return plane
 
         k1_l = load_list("k1_l", k1)
-        d_scale_tab = load_scale_rows("d_scale_tab", d_scales, G, nc.vector)
-        d_word_tab = load_words("d_word_tab", d_words, G)
         offs_l = load_list("offs_l", offs)
-        x_scale_tab = load_scale_rows("x_scale_tab", x_scales, T, nc.vector)
+        x_scale_tab = keep.tile([P, T], U8, name="x_scale_tab")
+        x_rows = x_scales[0].bitcast(I32)
+        nc.sync.dma_start(x_scale_tab[:].bitcast(I32), x_rows.unsqueeze(1).to_broadcast([K // QUAD, BLOCK_P, T // 4]))
+        d_scale_tab = keep.tile([P, G], U8, name="d_scale_tab", tag="d_scale_tab", align_bytes=64)
+        nc.vector.memset(d_scale_tab[:, :VECTOR_CLEARS].bitcast(I32), 0)
+        nc.gpsimd.memset(d_scale_tab[:, VECTOR_CLEARS:].bitcast(I32), 0)
+        nc.sync.dma_start(d_scale_tab[0:P:BLOCK_P, :].bitcast(I32), d_scales[0].bitcast(I32))
+        d_word_tab = load_words("d_word_tab", d_words, G)
         x_word_tab = load_words("x_word_tab", x_words, T)
         n1_l = load_list("n1_l", n1)
         n2_l = load_list("n2_l", n2)
-        cand_l = load_list("cand_l", cand)
-        n3_l = load_list("n3_l", n3)
-        n4_l = load_list("n4_l", n4)
-        n5_l = load_list("n5_l", n5)
         sl_t = load_rows("sl_t", sl)
         th_t = load_rows("th_t", th)
         gs_t = load_rows("gs_t", gs)
 
         first_bytes = keep.tile([P, H + S], U8, name="first_bytes", tag="first_bytes", align_bytes=64)
-        nc.vector.tensor_copy(first_bytes[:, :H], d_scale_tab[:].indirect(k1_l[:]))
         nc.vector.tensor_copy(first_bytes[:, H:], x_scale_tab[:].indirect(offs_l[:]))
+        nc.vector.tensor_copy(first_bytes[:, :H], d_scale_tab[:].indirect(k1_l[:]))
         first_plane = place_scale_rows("first_plane", first_bytes, H + S, nc.scalar)
+
+        cand_l = load_list("cand_l", cand)
+        n3_l = load_list("n3_l", n3)
+        n4_l = load_list("n4_l", n4)
+        n5_l = load_list("n5_l", n5)
 
         d_picked = keep.tile([P, H], U32, name="d_picked", tag="d_scale_tab", align_bytes=64)
         nc.vector.tensor_copy(d_picked[:], d_word_tab[:].indirect(k1_l[:]))
         x_picked = keep.tile([P, S], U32, name="x_picked", align_bytes=64)
 
+        def deal(name, tag, dtype, source, slots):
+            dealt = keep.tile([P, slots.stop - slots.start, P], dtype, name=name, tag=tag, align_bytes=64)
+            nc.vector.tensor_copy(dealt[:], source.rearrange("p (m t) -> p t m", t=PACK)[:, slots, :])
+            return dealt
+
         h, h_acc = [], []
-        for t in range(PACK):
-            d_dealt = keep.tile([P, P], U32, name=f"d_dealt{t}", align_bytes=64)
-            nc.vector.tensor_copy(d_dealt[:], d_picked[:, t:H:PACK])
-            if t == 0:
-                nc.vector.tensor_copy(x_picked[:], x_word_tab[:].indirect(offs_l[:]))
-            d_plane = keep.tile([P, P], U8, name=f"d_plane{t}", align_bytes=64)
-            nc.vector.tensor_copy(d_plane[:], first_plane[:, t:H:PACK])
+
+        def first_product(words, plane):
+            t = len(h)
             acc = psum.tile([P, S], F32, name=f"h_acc{t}", tag=f"h_acc{t}")
             nc.tensor.matmul_mx(
                 out=acc[:],
-                lhsT=d_dealt[:].bitcast(FP8X4),
-                lhsT_scale=d_plane[:],
+                lhsT=words.bitcast(FP8X4),
+                lhsT_scale=plane,
                 rhs=x_picked[:].bitcast(FP8X4),
                 rhs_scale=first_plane[:, H:],
                 start=True,
@@ -117,6 +119,17 @@ def tile_picked_pqhcerlswapd_none_p_kernel(
                 nc.vector.tensor_scalar(h_t[:], acc[:], SIXTEENTH, None, ALU.mult)
             h.append(h_t)
             h_acc.append(acc)
+
+        lead_words = deal("lead_words", "dealt_words", U32, d_picked[:], slice(0, 1))
+        nc.vector.tensor_copy(x_picked[:], x_word_tab[:].indirect(offs_l[:]))
+        lead_plane = deal("lead_plane", "lead_plane", U8, first_plane[:, :H], slice(0, 1))
+        first_product(lead_words[:, 0, :], lead_plane[:, 0, :])
+        rest_plane = deal("rest_plane", "rest_plane", U8, first_plane[:, :H], slice(1, PACK))
+        next_words = deal("next_words", "dealt_words", U32, d_picked[:], slice(1, 2))
+        first_product(next_words[:, 0, :], rest_plane[:, 0, :])
+        last_words = deal("last_words", "lead_plane", U32, d_picked[:], slice(2, PACK))
+        for t in range(2, PACK):
+            first_product(last_words[:, t - 2, :], rest_plane[:, t - 1, :])
 
         sl_th = keep.tile([P, PACK], F32, name="sl_th")
         nc.gpsimd.tensor_tensor(sl_th[:], sl_t[:], th_t[:], ALU.mult)
@@ -136,7 +149,7 @@ def tile_picked_pqhcerlswapd_none_p_kernel(
         cand_bytes = keep.tile([P, C], U8, name="cand_bytes", tag="first_plane", align_bytes=64)
         nc.vector.tensor_copy(cand_bytes[:], x_scale_tab[:].indirect(cand_l[:]))
         cand_plane = place_scale_rows("cand_plane", cand_bytes, C, nc.sync)
-        cand_picked = keep.tile([P, C], U32, name="cand_picked", tag="first_bytes", align_bytes=64)
+        cand_picked = keep.tile([P, C], U32, name="cand_picked", tag="rest_plane", align_bytes=64)
         nc.vector.tensor_copy(cand_picked[:], x_word_tab[:].indirect(cand_l[:]))
 
         tiles = C // P

@@ -71,6 +71,10 @@ def tile_picked_pqhcerlswapd_none_p_kernel(
         nc.vector.memset(d_scale_tab[:, :VECTOR_CLEARS].bitcast(I32), 0)
         nc.gpsimd.memset(d_scale_tab[:, VECTOR_CLEARS:].bitcast(I32), 0)
         nc.sync.dma_start(d_scale_tab[0:P:BLOCK_P, :].bitcast(I32), d_scales[0].bitcast(I32))
+        warm_in = keep.tile([P, 1], F32, name="warm_in")
+        nc.gpsimd.memset(warm_in[:], 0.0)
+        warm_out = keep.tile([P, 1], F32, name="warm_out")
+        nc.scalar.activation(warm_out[:], warm_in[:], ACT.Sigmoid)
         d_word_tab = load_words("d_word_tab", d_words, G)
         x_word_tab = load_words("x_word_tab", x_words, T)
         n1_l = load_list("n1_l", n1)

@@ -22,9 +22,10 @@ QUAD = 32
 PER_COL = 16
 HALF = S // 2
 SIXTEENTH = 0.0625
-DS_COLS = 352
+DS_COLS = 512
 DT_COLS = 264
 LAST = 64
+EARLY_WORDS = G // 8
 VECTOR_CLEARS = 3 * G // 4
 
 
@@ -62,11 +63,14 @@ def tile_picked_pqhcerlswapd_none_p_kernel(
                 queue.dma_start(plane[q : q + PACK, :].bitcast(I32), gathered[q : q + QUAD : BLOCK_P, :].bitcast(I32))
             return plane
 
-        k1_l = load_list("k1_l", k1)
-        offs_l = load_list("offs_l", offs)
         x_scale_tab = keep.tile([P, T], U8, name="x_scale_tab")
         x_rows = x_scales[0].bitcast(I32)
         nc.sync.dma_start(x_scale_tab[:].bitcast(I32), x_rows.unsqueeze(1).to_broadcast([K // QUAD, BLOCK_P, T // 4]))
+        offs_l = load_list("offs_l", offs)
+        k1_l = load_list("k1_l", k1)
+        d_word_tab = keep.tile([P, G], U32, name="d_word_tab")
+        d_word_rows = d_words[0].rearrange("p n t -> p (n t)").bitcast(I32)
+        nc.sync.dma_start(d_word_tab[:, :EARLY_WORDS].bitcast(I32), d_word_rows[:, :EARLY_WORDS])
         d_scale_tab = keep.tile([P, G], U8, name="d_scale_tab", tag="d_scale_tab", align_bytes=64)
         nc.vector.memset(d_scale_tab[:, :VECTOR_CLEARS].bitcast(I32), 0)
         nc.gpsimd.memset(d_scale_tab[:, VECTOR_CLEARS:].bitcast(I32), 0)
@@ -75,10 +79,9 @@ def tile_picked_pqhcerlswapd_none_p_kernel(
         nc.gpsimd.memset(warm_in[:], 0.0)
         warm_out = keep.tile([P, 1], F32, name="warm_out")
         nc.scalar.activation(warm_out[:], warm_in[:], ACT.Sigmoid)
-        d_word_tab = load_words("d_word_tab", d_words, G)
+        nc.sync.dma_start(d_word_tab[:, EARLY_WORDS:].bitcast(I32), d_word_rows[:, EARLY_WORDS:])
         x_word_tab = load_words("x_word_tab", x_words, T)
         n1_l = load_list("n1_l", n1)
-        n2_l = load_list("n2_l", n2)
         sl_t = load_rows("sl_t", sl)
         th_t = load_rows("th_t", th)
         gs_t = load_rows("gs_t", gs)
@@ -88,52 +91,63 @@ def tile_picked_pqhcerlswapd_none_p_kernel(
         nc.vector.tensor_copy(first_bytes[:, :H], d_scale_tab[:].indirect(k1_l[:]))
         first_plane = place_scale_rows("first_plane", first_bytes, H + S, nc.scalar)
 
+        n2_l = load_list("n2_l", n2)
         cand_l = load_list("cand_l", cand)
         n3_l = load_list("n3_l", n3)
         n4_l = load_list("n4_l", n4)
-        n5_l = load_list("n5_l", n5)
 
         d_picked = keep.tile([P, H], U32, name="d_picked", tag="d_scale_tab", align_bytes=64)
         nc.vector.tensor_copy(d_picked[:], d_word_tab[:].indirect(k1_l[:]))
-        x_picked = keep.tile([P, S], U32, name="x_picked", align_bytes=64)
 
         def deal(name, tag, dtype, source, slots):
             dealt = keep.tile([P, slots.stop - slots.start, P], dtype, name=name, tag=tag, align_bytes=64)
             nc.vector.tensor_copy(dealt[:], source.rearrange("p (m t) -> p t m", t=PACK)[:, slots, :])
             return dealt
 
-        h, h_acc = [], []
+        h = [keep.tile([P, S], F32, name=f"h{t}", tag=f"h{t}", align_bytes=64) for t in range(PACK)]
+        ds = [keep.tile([P, DS_COLS], F32, name=f"ds{t}") for t in range(PACK)]
+        x_picked = {}
+        h_acc = []
 
-        def first_product(words, plane):
-            t = len(h)
-            acc = psum.tile([P, S], F32, name=f"h_acc{t}", tag=f"h_acc{t}")
-            nc.tensor.matmul_mx(
-                out=acc[:],
-                lhsT=words.bitcast(FP8X4),
-                lhsT_scale=plane,
-                rhs=x_picked[:].bitcast(FP8X4),
-                rhs_scale=first_plane[:, H:],
-                start=True,
-                stop=True,
-            )
-            h_t = keep.tile([P, S], F32, name=f"h{t}", tag=f"h{t}")
-            if t == 0:
-                nc.scalar.activation(h_t[:], acc[:], ACT.Copy, scale=SIXTEENTH)
-            else:
-                nc.vector.tensor_scalar(h_t[:], acc[:], SIXTEENTH, None, ALU.mult)
-            h.append(h_t)
-            h_acc.append(acc)
+        def pick_tokens(j0, tag):
+            x_picked[j0] = keep.tile([P, HALF], U32, name=f"x_picked{j0}", tag=tag, align_bytes=64)
+            nc.vector.tensor_copy(x_picked[j0][:], x_word_tab[:].indirect(entries(offs_l, j0, HALF)))
 
-        lead_words = deal("lead_words", "dealt_words", U32, d_picked[:], slice(0, 1))
-        nc.vector.tensor_copy(x_picked[:], x_word_tab[:].indirect(offs_l[:]))
+        def first_product(t, words, plane, first, count, emptying):
+            acc = psum.tile([P, count], F32, name=f"h_acc{len(h_acc)}", tag=f"h_acc{len(h_acc)}")
+            for j0 in range(first, first + count, HALF):
+                nc.tensor.matmul_mx(
+                    out=acc[:, j0 - first : j0 - first + HALF],
+                    lhsT=words.bitcast(FP8X4),
+                    lhsT_scale=plane,
+                    rhs=x_picked[j0][:].bitcast(FP8X4),
+                    rhs_scale=first_plane[:, H + j0 : H + j0 + HALF],
+                    start=True,
+                    stop=True,
+                )
+            cols = slice(first, first + count)
+            emptying(h[t][:, cols], acc[:])
+            nc.scalar.activation(ds[t][:].indirect(entries(n1_l, first, count)), h[t][:, cols], ACT.Copy)
+            h_acc.append((t, cols, acc))
+
+        def sixteenth_on_scalar(to, bank):
+            nc.scalar.activation(to, bank, ACT.Copy, scale=SIXTEENTH)
+
+        def sixteenth_on_vector(to, bank):
+            nc.vector.tensor_scalar(to, bank, SIXTEENTH, None, ALU.mult)
+
+        lead_words = deal("lead_words", "lead_words", U32, d_picked[:], slice(0, 1))
+        pick_tokens(0, "x_picked")
         lead_plane = deal("lead_plane", "lead_plane", U8, first_plane[:, :H], slice(0, 1))
-        first_product(lead_words[:, 0, :], lead_plane[:, 0, :])
+        first_product(0, lead_words[:, 0, :], lead_plane[:, 0, :], 0, HALF, sixteenth_on_scalar)
+        pick_tokens(HALF, "first_bytes")
+        first_product(0, lead_words[:, 0, :], lead_plane[:, 0, :], HALF, HALF, sixteenth_on_vector)
         rest_plane = deal("rest_plane", "rest_plane", U8, first_plane[:, :H], slice(1, PACK))
-        next_words = deal("next_words", "dealt_words", U32, d_picked[:], slice(1, 2))
-        first_product(next_words[:, 0, :], rest_plane[:, 0, :])
+        next_words = deal("next_words", "lead_words", U32, d_picked[:], slice(1, 2))
+        first_product(1, next_words[:, 0, :], rest_plane[:, 0, :], 0, S, sixteenth_on_vector)
         last_words = deal("last_words", "lead_plane", U32, d_picked[:], slice(2, PACK))
         for t in range(2, PACK):
-            first_product(last_words[:, t - 2, :], rest_plane[:, t - 1, :])
+            first_product(t, last_words[:, t - 2, :], rest_plane[:, t - 1, :], 0, S, sixteenth_on_vector)
 
         sl_th = keep.tile([P, PACK], F32, name="sl_th")
         nc.gpsimd.tensor_tensor(sl_th[:], sl_t[:], th_t[:], ALU.mult)
@@ -141,61 +155,65 @@ def tile_picked_pqhcerlswapd_none_p_kernel(
         nc.gpsimd.tensor_scalar(bias[:], sl_th[:], -1.0, 0.0, ALU.mult, ALU.add)
 
         hg = keep.tile([P, PACK, S], F32, name="hg")
-        for t in range(PACK):
-            nc.vector.tensor_scalar(hg[:, t, :], h_acc[t][:], gs_t[:, t : t + 1], SIXTEENTH, ALU.mult, ALU.mult)
+        for t, cols, acc in h_acc:
+            nc.vector.tensor_scalar(hg[:, t, cols], acc[:], gs_t[:, t : t + 1], SIXTEENTH, ALU.mult, ALU.mult)
 
-        ds = []
-        for t in range(PACK):
-            ds_t = keep.tile([P, DS_COLS], F32, name=f"ds{t}")
-            nc.scalar.activation(ds_t[:].indirect(n1_l[:]), h[t][:], ACT.Copy)
-            ds.append(ds_t)
-
-        cand_bytes = keep.tile([P, C], U8, name="cand_bytes", tag="first_plane", align_bytes=64)
+        cand_bytes = keep.tile([P, C], U8, name="cand_bytes", tag="h1", align_bytes=64)
         nc.vector.tensor_copy(cand_bytes[:], x_scale_tab[:].indirect(cand_l[:]))
         cand_plane = place_scale_rows("cand_plane", cand_bytes, C, nc.sync)
-        cand_picked = keep.tile([P, C], U32, name="cand_picked", tag="rest_plane", align_bytes=64)
+        n5_l = load_list("n5_l", n5)
+        cand_picked = keep.tile([P, C], U32, name="cand_picked", tag="h2", align_bytes=64)
         nc.vector.tensor_copy(cand_picked[:], x_word_tab[:].indirect(cand_l[:]))
 
         tiles = C // P
         s = [keep.tile([P, S], F32, name=f"s{u}") for u in range(tiles)]
-        sg = keep.tile([P, PACK, S], F32, name="sg", tag=f"h{PACK - 1}")
-        s_acc = {}
+        sg = keep.tile([P, PACK, S], F32, name="sg", tag=f"h{PACK - 1}", align_bytes=64)
+        z_woven = keep.tile([P, S, PACK], BF16, name="z_woven", align_bytes=64)
+
+        def fetch_gate(t, j0, width):
+            nc.scalar.activation(
+                sg[:, t, j0 : j0 + width], ds[t][:].indirect(entries(n2_l, j0, width)), ACT.Sigmoid,
+                bias=bias[:, t : t + 1], scale=sl_t[:, t : t + 1],
+            )
+
+        def weave_pair(t, j0, width):
+            cols, pair = slice(j0, j0 + width), slice(t, t + 2)
+            nc.vector.tensor_tensor(
+                z_woven[:, cols, pair],
+                hg[:, pair, cols].rearrange("p t j -> p j t"),
+                sg[:, pair, cols].rearrange("p t j -> p j t"),
+                ALU.mult,
+            )
+
+        fetch_gate(0, 0, S)
+        fetch_gate(1, 0, S)
+        weave_pair(0, 0, S)
+        fetch_gate(2, 0, S)
+        for j0 in range(0, S, HALF):
+            fetch_gate(3, j0, HALF)
+            weave_pair(2, j0, HALF)
+        z_words = keep.tile([P, S], U32, name="z_words", align_bytes=64)
+        z_plane = keep.tile([P, S], U8, name="z_plane", align_bytes=64)
         for j0 in range(0, S, HALF):
             cols = slice(j0, j0 + HALF)
-            z_woven = keep.tile([P, HALF, PACK], BF16, name=f"z_woven{j0}", tag="z_woven", align_bytes=64)
-            for t in range(PACK):
-                nc.scalar.activation(
-                    sg[:, t, cols], ds[t][:].indirect(entries(n2_l, j0, HALF)), ACT.Sigmoid,
-                    bias=bias[:, t : t + 1], scale=sl_t[:, t : t + 1],
-                )
-                if t % 2 == 1:
-                    pair = slice(t - 1, t + 1)
-                    nc.vector.tensor_tensor(
-                        z_woven[:, :, pair],
-                        hg[:, pair, cols].rearrange("p t j -> p j t"),
-                        sg[:, pair, cols].rearrange("p t j -> p j t"),
-                        ALU.mult,
-                    )
-            z_words = keep.tile([P, HALF], U32, name=f"z_words{j0}", align_bytes=64)
-            z_plane = keep.tile([P, HALF], U8, name=f"z_plane{j0}", align_bytes=64)
-            nc.vector.quantize_mx(z_words[:].bitcast(FP8X4), z_plane[:], z_woven[:].rearrange("p j t -> p (j t)"))
-            for u in range(tiles):
-                rows = slice(u * P, (u + 1) * P)
-                s_acc[u, j0] = psum.tile([P, HALF], F32, name=f"s_acc{u}_{j0}", tag=f"s_acc{u}" if j0 == 0 else f"h_acc{u}")
+            nc.vector.quantize_mx(z_words[:, cols].bitcast(FP8X4), z_plane[:, cols], z_woven[:, cols, :].rearrange("p j t -> p (j t)"))
+        for u in range(tiles):
+            rows = slice(u * P, (u + 1) * P)
+            for j0 in range(0, S, HALF):
+                cols = slice(j0, j0 + HALF)
+                bank = 2 * u + j0 // HALF
+                s_acc = psum.tile([P, HALF], F32, name=f"s_acc{bank}", tag=f"h_acc{bank}")
                 nc.tensor.matmul_mx(
-                    out=s_acc[u, j0][:],
+                    out=s_acc[:],
                     lhsT=cand_picked[:, rows].bitcast(FP8X4),
                     lhsT_scale=cand_plane[:, rows],
-                    rhs=z_words[:].bitcast(FP8X4),
-                    rhs_scale=z_plane[:],
+                    rhs=z_words[:, cols].bitcast(FP8X4),
+                    rhs_scale=z_plane[:, cols],
                     start=True,
                     stop=True,
                 )
-        for u in range(tiles):
-            nc.scalar.activation(s[u][:, :HALF], s_acc[u, 0][:], ACT.Copy, scale=SIXTEENTH)
-        nc.scalar.activation(s[0][:, HALF:], s_acc[0, HALF][:], ACT.Copy, scale=SIXTEENTH)
-        for u in range(1, tiles):
-            nc.vector.tensor_scalar(s[u][:, HALF:], s_acc[u, HALF][:], SIXTEENTH, None, ALU.mult)
+                emptying = sixteenth_on_scalar if u == 0 else sixteenth_on_vector
+                emptying(s[u][:, cols], s_acc[:])
 
         pb, rb, dt = {}, {}, {}
 

@@ -17,14 +17,19 @@ ALU = mybir.AluOpType
 
 P = 128
 PACK = 4
-BLOCK_P = 8
+BLOCK = 32
+BLOCK_P = BLOCK // PACK
 QUAD = 32
 PER_COL = 16
 HALF = S // 2
+PAIR = 2
+TILES = C // P
 SIXTEENTH = 0.0625
-DS_COLS = 512
-DT_COLS = 264
-LAST = 64
+MX_ALIGN = 64
+
+DS_COLS = 2 * S
+DT_COLS = S + 8
+LAST = S // 4
 EARLY_WORDS = G // 8
 VECTOR_CLEARS = 3 * G // 4
 
@@ -46,47 +51,49 @@ def tile_picked_pqhcerlswapd_none_p_kernel(
         def entries(held, first, count):
             return held[:, first // PER_COL : (first + count) // PER_COL]
 
-        def load_words(name, src, cols):
-            held = keep.tile([P, cols], U32, name=name)
-            nc.sync.dma_start(held[:].bitcast(I32), src[0].rearrange("p n t -> p (n t)").bitcast(I32))
-            return held
+        def word_rows(words):
+            return words[0].rearrange("p n t -> p (n t)").bitcast(I32)
 
-        def load_rows(name, src):
+        def load_row_values(name, src):
             held = keep.tile([P, PACK], F32, name=name)
             nc.gpsimd.dma_start(held[:], src.rearrange("(p t) o -> p (t o)", t=PACK))
             return held
 
         def place_scale_rows(name, gathered, cols, queue):
-            plane = keep.tile([P, cols], U8, name=name, tag=name, align_bytes=64)
+            plane = keep.tile([P, cols], U8, name=name, tag=name, align_bytes=MX_ALIGN)
             nc.vector.memset(plane[:].bitcast(I32), 0)
             for q in range(0, P, QUAD):
                 queue.dma_start(plane[q : q + PACK, :].bitcast(I32), gathered[q : q + QUAD : BLOCK_P, :].bitcast(I32))
             return plane
 
-        x_scale_tab = keep.tile([P, T], U8, name="x_scale_tab")
-        x_rows = x_scales[0].bitcast(I32)
-        nc.sync.dma_start(x_scale_tab[:].bitcast(I32), x_rows.unsqueeze(1).to_broadcast([K // QUAD, BLOCK_P, T // 4]))
+        x_scale_tab = keep.tile([P, T], U8, name="x_scale_tab", tag="x_scale_tab", align_bytes=MX_ALIGN)
+        x_scale_rows = x_scales[0].bitcast(I32)
+        nc.sync.dma_start(
+            x_scale_tab[:].bitcast(I32), x_scale_rows.unsqueeze(1).to_broadcast([K // BLOCK, BLOCK_P, x_scale_rows.shape[1]])
+        )
         offs_l = load_list("offs_l", offs)
         k1_l = load_list("k1_l", k1)
         d_word_tab = keep.tile([P, G], U32, name="d_word_tab")
-        d_word_rows = d_words[0].rearrange("p n t -> p (n t)").bitcast(I32)
-        nc.sync.dma_start(d_word_tab[:, :EARLY_WORDS].bitcast(I32), d_word_rows[:, :EARLY_WORDS])
-        d_scale_tab = keep.tile([P, G], U8, name="d_scale_tab", tag="d_scale_tab", align_bytes=64)
+        nc.sync.dma_start(d_word_tab[:, :EARLY_WORDS].bitcast(I32), word_rows(d_words)[:, :EARLY_WORDS])
+        d_scale_tab = keep.tile([P, G], U8, name="d_scale_tab", tag="d_scale_tab", align_bytes=MX_ALIGN)
         nc.vector.memset(d_scale_tab[:, :VECTOR_CLEARS].bitcast(I32), 0)
         nc.gpsimd.memset(d_scale_tab[:, VECTOR_CLEARS:].bitcast(I32), 0)
         nc.sync.dma_start(d_scale_tab[0:P:BLOCK_P, :].bitcast(I32), d_scales[0].bitcast(I32))
+
         warm_in = keep.tile([P, 1], F32, name="warm_in")
         nc.gpsimd.memset(warm_in[:], 0.0)
         warm_out = keep.tile([P, 1], F32, name="warm_out")
         nc.scalar.activation(warm_out[:], warm_in[:], ACT.Sigmoid)
-        nc.sync.dma_start(d_word_tab[:, EARLY_WORDS:].bitcast(I32), d_word_rows[:, EARLY_WORDS:])
-        x_word_tab = load_words("x_word_tab", x_words, T)
-        n1_l = load_list("n1_l", n1)
-        sl_t = load_rows("sl_t", sl)
-        th_t = load_rows("th_t", th)
-        gs_t = load_rows("gs_t", gs)
 
-        first_bytes = keep.tile([P, H + S], U8, name="first_bytes", tag="first_bytes", align_bytes=64)
+        nc.sync.dma_start(d_word_tab[:, EARLY_WORDS:].bitcast(I32), word_rows(d_words)[:, EARLY_WORDS:])
+        x_word_tab = keep.tile([P, T], U32, name="x_word_tab")
+        nc.sync.dma_start(x_word_tab[:].bitcast(I32), word_rows(x_words))
+        n1_l = load_list("n1_l", n1)
+        sl_t = load_row_values("sl_t", sl)
+        th_t = load_row_values("th_t", th)
+        gs_t = load_row_values("gs_t", gs)
+
+        first_bytes = keep.tile([P, H + S], U8, name="first_bytes", tag="first_bytes", align_bytes=MX_ALIGN)
         nc.vector.tensor_copy(first_bytes[:, H:], x_scale_tab[:].indirect(offs_l[:]))
         nc.vector.tensor_copy(first_bytes[:, :H], d_scale_tab[:].indirect(k1_l[:]))
         first_plane = place_scale_rows("first_plane", first_bytes, H + S, nc.scalar)
@@ -96,25 +103,25 @@ def tile_picked_pqhcerlswapd_none_p_kernel(
         n3_l = load_list("n3_l", n3)
         n4_l = load_list("n4_l", n4)
 
-        d_picked = keep.tile([P, H], U32, name="d_picked", tag="d_scale_tab", align_bytes=64)
+        d_picked = keep.tile([P, H], U32, name="d_picked", tag="d_scale_tab", align_bytes=MX_ALIGN)
         nc.vector.tensor_copy(d_picked[:], d_word_tab[:].indirect(k1_l[:]))
 
         def deal(name, tag, dtype, source, slots):
-            dealt = keep.tile([P, slots.stop - slots.start, P], dtype, name=name, tag=tag, align_bytes=64)
+            dealt = keep.tile([P, slots.stop - slots.start, P], dtype, name=name, tag=tag, align_bytes=MX_ALIGN)
             nc.vector.tensor_copy(dealt[:], source.rearrange("p (m t) -> p t m", t=PACK)[:, slots, :])
             return dealt
 
-        h = [keep.tile([P, S], F32, name=f"h{t}", tag=f"h{t}", align_bytes=64) for t in range(PACK)]
+        h = [keep.tile([P, S], F32, name=f"h{t}", tag=f"h{t}", align_bytes=MX_ALIGN) for t in range(PACK)]
         ds = [keep.tile([P, DS_COLS], F32, name=f"ds{t}") for t in range(PACK)]
         x_picked = {}
-        h_acc = []
+        h_banks = []
 
         def pick_tokens(j0, tag):
-            x_picked[j0] = keep.tile([P, HALF], U32, name=f"x_picked{j0}", tag=tag, align_bytes=64)
+            x_picked[j0] = keep.tile([P, HALF], U32, name=f"x_picked{j0}", tag=tag, align_bytes=MX_ALIGN)
             nc.vector.tensor_copy(x_picked[j0][:], x_word_tab[:].indirect(entries(offs_l, j0, HALF)))
 
         def first_product(t, words, plane, first, count, emptying):
-            acc = psum.tile([P, count], F32, name=f"h_acc{len(h_acc)}", tag=f"h_acc{len(h_acc)}")
+            acc = psum.tile([P, count], F32, name=f"h_acc{len(h_banks)}", tag=f"bank{len(h_banks)}")
             for j0 in range(first, first + count, HALF):
                 nc.tensor.matmul_mx(
                     out=acc[:, j0 - first : j0 - first + HALF],
@@ -127,27 +134,33 @@ def tile_picked_pqhcerlswapd_none_p_kernel(
                 )
             cols = slice(first, first + count)
             emptying(h[t][:, cols], acc[:])
-            nc.scalar.activation(ds[t][:].indirect(entries(n1_l, first, count)), h[t][:, cols], ACT.Copy)
-            h_acc.append((t, cols, acc))
+            h_banks.append((t, cols, acc))
 
-        def sixteenth_on_scalar(to, bank):
-            nc.scalar.activation(to, bank, ACT.Copy, scale=SIXTEENTH)
+        def put_h(t, first, count):
+            nc.scalar.activation(ds[t][:].indirect(entries(n1_l, first, count)), h[t][:, first : first + count], ACT.Copy)
 
-        def sixteenth_on_vector(to, bank):
-            nc.vector.tensor_scalar(to, bank, SIXTEENTH, None, ALU.mult)
+        def sixteenth_on_scalar(to, acc):
+            nc.scalar.activation(to, acc, ACT.Copy, scale=SIXTEENTH)
+
+        def sixteenth_on_vector(to, acc):
+            nc.vector.tensor_scalar(to, acc, SIXTEENTH, None, ALU.mult)
 
         lead_words = deal("lead_words", "lead_words", U32, d_picked[:], slice(0, 1))
         pick_tokens(0, "x_picked")
         lead_plane = deal("lead_plane", "lead_plane", U8, first_plane[:, :H], slice(0, 1))
         first_product(0, lead_words[:, 0, :], lead_plane[:, 0, :], 0, HALF, sixteenth_on_scalar)
+        put_h(0, 0, HALF)
         pick_tokens(HALF, "first_bytes")
         first_product(0, lead_words[:, 0, :], lead_plane[:, 0, :], HALF, HALF, sixteenth_on_vector)
+        put_h(0, HALF, HALF)
         rest_plane = deal("rest_plane", "rest_plane", U8, first_plane[:, :H], slice(1, PACK))
         next_words = deal("next_words", "lead_words", U32, d_picked[:], slice(1, 2))
         first_product(1, next_words[:, 0, :], rest_plane[:, 0, :], 0, S, sixteenth_on_vector)
+        put_h(1, 0, S)
         last_words = deal("last_words", "lead_plane", U32, d_picked[:], slice(2, PACK))
         for t in range(2, PACK):
             first_product(t, last_words[:, t - 2, :], rest_plane[:, t - 1, :], 0, S, sixteenth_on_vector)
+        put_h(2, 0, S)
 
         sl_th = keep.tile([P, PACK], F32, name="sl_th")
         nc.gpsimd.tensor_tensor(sl_th[:], sl_t[:], th_t[:], ALU.mult)
@@ -155,54 +168,59 @@ def tile_picked_pqhcerlswapd_none_p_kernel(
         nc.gpsimd.tensor_scalar(bias[:], sl_th[:], -1.0, 0.0, ALU.mult, ALU.add)
 
         hg = keep.tile([P, PACK, S], F32, name="hg")
-        for t, cols, acc in h_acc:
+        for t, cols, acc in h_banks:
             nc.vector.tensor_scalar(hg[:, t, cols], acc[:], gs_t[:, t : t + 1], SIXTEENTH, ALU.mult, ALU.mult)
 
-        cand_bytes = keep.tile([P, C], U8, name="cand_bytes", tag="h1", align_bytes=64)
+        cand_bytes = keep.tile([P, C], U8, name="cand_bytes", tag="h2", align_bytes=MX_ALIGN)
         nc.vector.tensor_copy(cand_bytes[:], x_scale_tab[:].indirect(cand_l[:]))
         cand_plane = place_scale_rows("cand_plane", cand_bytes, C, nc.sync)
         n5_l = load_list("n5_l", n5)
-        cand_picked = keep.tile([P, C], U32, name="cand_picked", tag="h2", align_bytes=64)
+        cand_picked = keep.tile([P, C], U32, name="cand_picked", tag="x_scale_tab", align_bytes=MX_ALIGN)
         nc.vector.tensor_copy(cand_picked[:], x_word_tab[:].indirect(cand_l[:]))
 
-        tiles = C // P
-        s = [keep.tile([P, S], F32, name=f"s{u}") for u in range(tiles)]
-        sg = keep.tile([P, PACK, S], F32, name="sg", tag=f"h{PACK - 1}", align_bytes=64)
-        z_woven = keep.tile([P, S, PACK], BF16, name="z_woven", align_bytes=64)
+        s = [keep.tile([P, S], F32, name=f"s{u}") for u in range(TILES)]
+        sg = [keep.tile([P, PAIR, S], F32, name=f"sg{t}", tag=f"h{t + 1}", align_bytes=MX_ALIGN) for t in range(0, PACK, PAIR)]
+        z_woven = keep.tile([P, S, PACK], BF16, name="z_woven", align_bytes=MX_ALIGN)
 
         def fetch_gate(t, j0, width):
             nc.scalar.activation(
-                sg[:, t, j0 : j0 + width], ds[t][:].indirect(entries(n2_l, j0, width)), ACT.Sigmoid,
-                bias=bias[:, t : t + 1], scale=sl_t[:, t : t + 1],
+                sg[t // PAIR][:, t % PAIR, j0 : j0 + width],
+                ds[t][:].indirect(entries(n2_l, j0, width)),
+                ACT.Sigmoid,
+                bias=bias[:, t : t + 1],
+                scale=sl_t[:, t : t + 1],
             )
 
         def weave_pair(t, j0, width):
-            cols, pair = slice(j0, j0 + width), slice(t, t + 2)
+            cols, pair = slice(j0, j0 + width), slice(t, t + PAIR)
             nc.vector.tensor_tensor(
                 z_woven[:, cols, pair],
                 hg[:, pair, cols].rearrange("p t j -> p j t"),
-                sg[:, pair, cols].rearrange("p t j -> p j t"),
+                sg[t // PAIR][:, :, cols].rearrange("p t j -> p j t"),
                 ALU.mult,
             )
 
         fetch_gate(0, 0, S)
         fetch_gate(1, 0, S)
+        put_h(3, 0, S)
         weave_pair(0, 0, S)
         fetch_gate(2, 0, S)
         for j0 in range(0, S, HALF):
             fetch_gate(3, j0, HALF)
             weave_pair(2, j0, HALF)
-        z_words = keep.tile([P, S], U32, name="z_words", align_bytes=64)
-        z_plane = keep.tile([P, S], U8, name="z_plane", align_bytes=64)
+        z_words = keep.tile([P, S], U32, name="z_words", align_bytes=MX_ALIGN)
+        z_plane = keep.tile([P, S], U8, name="z_plane", align_bytes=MX_ALIGN)
         for j0 in range(0, S, HALF):
             cols = slice(j0, j0 + HALF)
-            nc.vector.quantize_mx(z_words[:, cols].bitcast(FP8X4), z_plane[:, cols], z_woven[:, cols, :].rearrange("p j t -> p (j t)"))
-        for u in range(tiles):
+            nc.vector.quantize_mx(
+                z_words[:, cols].bitcast(FP8X4), z_plane[:, cols], z_woven[:, cols, :].rearrange("p j t -> p (j t)")
+            )
+        for u in range(TILES):
             rows = slice(u * P, (u + 1) * P)
             for j0 in range(0, S, HALF):
                 cols = slice(j0, j0 + HALF)
-                bank = 2 * u + j0 // HALF
-                s_acc = psum.tile([P, HALF], F32, name=f"s_acc{bank}", tag=f"h_acc{bank}")
+                bank = (u * S + j0) // HALF
+                s_acc = psum.tile([P, HALF], F32, name=f"s_acc{bank}", tag=f"bank{bank}")
                 nc.tensor.matmul_mx(
                     out=s_acc[:],
                     lhsT=cand_picked[:, rows].bitcast(FP8X4),
@@ -232,7 +250,8 @@ def tile_picked_pqhcerlswapd_none_p_kernel(
         def put_rb(u):
             nc.scalar.activation(dt[u][:].indirect(n4_l[:]), rb[u][:], ACT.Copy)
 
-        def finish(u, pieces):
+        def finish(u):
+            pieces = [(0, S - LAST), (S - LAST, LAST)] if u == TILES - 1 else [(0, S)]
             for j0, width in pieces:
                 cols = slice(j0, j0 + width)
                 other = keep.tile([P, width], F32, name=f"other{u}_{j0}")
@@ -241,12 +260,8 @@ def tile_picked_pqhcerlswapd_none_p_kernel(
                 nc.vector.scalar_tensor_tensor(result[:], other[:], 0.5, dt[u][:, cols], ALU.mult, ALU.max)
                 nc.sync.dma_start(out[u * P : (u + 1) * P, cols], result[:])
 
-        for step in range(tiles + 3):
-            if step < tiles:
-                fetch_pairs(step)
-            if 2 <= step < tiles + 2:
-                put_rb(step - 2)
-            if 1 <= step < tiles + 1:
-                put_pb(step - 1)
-            if step >= 3:
-                finish(step - 3, [(0, S - LAST), (S - LAST, LAST)] if step - 3 == tiles - 1 else [(0, S)])
+        stages = [(fetch_pairs, 0), (put_rb, 2), (put_pb, 1), (finish, 3)]
+        for step in range(TILES + len(stages) - 1):
+            for f, lag in stages:
+                if 0 <= step - lag < TILES:
+                    f(step - lag)

from contextlib import ExitStack

import concourse.mybir as mybir

K, T, S, G, H, C, W = 512, 1024, 256, 2048, 512, 512, 128
FLOPS = 2 * K * H * S + 2 * K * C * S

F32 = mybir.dt.float32
BF16 = mybir.dt.bfloat16
I32 = mybir.dt.int32
U32 = mybir.dt.uint32
U16 = mybir.dt.uint16
U8 = mybir.dt.uint8
FP8X4 = mybir.dt.float8_e4m3fn_x4
ACT = mybir.ActivationFunctionType
ALU = mybir.AluOpType

P = 128
PACK = 4
BLOCK = 32
BLOCK_P = BLOCK // PACK
QUAD = 32
PER_COL = 16
HALF = S // 2
PAIR = 2
TILES = C // P
SIXTEENTH = 0.0625
MX_ALIGN = 64

DS_COLS = 2 * S
DT_COLS = S + 8
LAST = S // 4
EARLY_WORDS = G // 8
VECTOR_CLEARS = 3 * G // 4


def tile_picked_pqhcerlswapd_none_p_kernel(
    tc, x_words, x_scales, d_words, d_scales, sl, th, gs, offs, k1, n1, n2, cand, n3, n4, n5, out
):
    nc = tc.nc
    with ExitStack() as ctx:
        lists = ctx.enter_context(tc.tile_pool(name="lists", bufs=1))
        keep = ctx.enter_context(tc.tile_pool(name="keep", bufs=1))
        psum = ctx.enter_context(tc.psum_pool(name="psum", bufs=1))

        def load_list(name, src):
            held = lists.tile(list(src.shape), U16, name=name)
            nc.sync.dma_start(held[:], src)
            return held

        def entries(held, first, count):
            return held[:, first // PER_COL : (first + count) // PER_COL]

        def word_rows(words):
            return words[0].rearrange("p n t -> p (n t)").bitcast(I32)

        def load_row_values(name, src):
            held = keep.tile([P, PACK], F32, name=name)
            nc.gpsimd.dma_start(held[:], src.rearrange("(p t) o -> p (t o)", t=PACK))
            return held

        def place_scale_rows(name, gathered, cols, queue):
            plane = keep.tile([P, cols], U8, name=name, tag=name, align_bytes=MX_ALIGN)
            nc.vector.memset(plane[:].bitcast(I32), 0)
            for q in range(0, P, QUAD):
                queue.dma_start(plane[q : q + PACK, :].bitcast(I32), gathered[q : q + QUAD : BLOCK_P, :].bitcast(I32))
            return plane

        x_scale_tab = keep.tile([P, T], U8, name="x_scale_tab", tag="x_scale_tab", align_bytes=MX_ALIGN)
        x_scale_rows = x_scales[0].bitcast(I32)
        nc.sync.dma_start(
            x_scale_tab[:].bitcast(I32), x_scale_rows.unsqueeze(1).to_broadcast([K // BLOCK, BLOCK_P, x_scale_rows.shape[1]])
        )
        offs_l = load_list("offs_l", offs)
        k1_l = load_list("k1_l", k1)
        d_word_tab = keep.tile([P, G], U32, name="d_word_tab")
        nc.sync.dma_start(d_word_tab[:, :EARLY_WORDS].bitcast(I32), word_rows(d_words)[:, :EARLY_WORDS])
        d_scale_tab = keep.tile([P, G], U8, name="d_scale_tab", tag="d_scale_tab", align_bytes=MX_ALIGN)
        nc.vector.memset(d_scale_tab[:, :VECTOR_CLEARS].bitcast(I32), 0)
        nc.gpsimd.memset(d_scale_tab[:, VECTOR_CLEARS:].bitcast(I32), 0)
        nc.sync.dma_start(d_scale_tab[0:P:BLOCK_P, :].bitcast(I32), d_scales[0].bitcast(I32))

        warm_in = keep.tile([P, 1], F32, name="warm_in")
        nc.gpsimd.memset(warm_in[:], 0.0)
        warm_out = keep.tile([P, 1], F32, name="warm_out")
        nc.scalar.activation(warm_out[:], warm_in[:], ACT.Sigmoid)

        nc.sync.dma_start(d_word_tab[:, EARLY_WORDS:].bitcast(I32), word_rows(d_words)[:, EARLY_WORDS:])
        x_word_tab = keep.tile([P, T], U32, name="x_word_tab")
        nc.sync.dma_start(x_word_tab[:].bitcast(I32), word_rows(x_words))
        n1_l = load_list("n1_l", n1)
        sl_t = load_row_values("sl_t", sl)
        th_t = load_row_values("th_t", th)
        gs_t = load_row_values("gs_t", gs)

        first_bytes = keep.tile([P, H + S], U8, name="first_bytes", tag="first_bytes", align_bytes=MX_ALIGN)
        nc.vector.tensor_copy(first_bytes[:, H:], x_scale_tab[:].indirect(offs_l[:]))
        nc.vector.tensor_copy(first_bytes[:, :H], d_scale_tab[:].indirect(k1_l[:]))
        first_plane = place_scale_rows("first_plane", first_bytes, H + S, nc.scalar)

        n2_l = load_list("n2_l", n2)
        cand_l = load_list("cand_l", cand)
        n3_l = load_list("n3_l", n3)
        n4_l = load_list("n4_l", n4)

        d_picked = keep.tile([P, H], U32, name="d_picked", tag="d_scale_tab", align_bytes=MX_ALIGN)
        nc.vector.tensor_copy(d_picked[:], d_word_tab[:].indirect(k1_l[:]))

        def deal(name, tag, dtype, source, slots):
            dealt = keep.tile([P, slots.stop - slots.start, P], dtype, name=name, tag=tag, align_bytes=MX_ALIGN)
            nc.vector.tensor_copy(dealt[:], source.rearrange("p (m t) -> p t m", t=PACK)[:, slots, :])
            return dealt

        h = [keep.tile([P, S], F32, name=f"h{t}", tag=f"h{t}", align_bytes=MX_ALIGN) for t in range(PACK)]
        ds = [keep.tile([P, DS_COLS], F32, name=f"ds{t}") for t in range(PACK)]
        x_picked = {}
        h_banks = []

        def pick_tokens(j0, tag):
            x_picked[j0] = keep.tile([P, HALF], U32, name=f"x_picked{j0}", tag=tag, align_bytes=MX_ALIGN)
            nc.vector.tensor_copy(x_picked[j0][:], x_word_tab[:].indirect(entries(offs_l, j0, HALF)))

        def first_product(t, words, plane, first, count, emptying):
            acc = psum.tile([P, count], F32, name=f"h_acc{len(h_banks)}", tag=f"bank{len(h_banks)}")
            for j0 in range(first, first + count, HALF):
                nc.tensor.matmul_mx(
                    out=acc[:, j0 - first : j0 - first + HALF],
                    lhsT=words.bitcast(FP8X4),
                    lhsT_scale=plane,
                    rhs=x_picked[j0][:].bitcast(FP8X4),
                    rhs_scale=first_plane[:, H + j0 : H + j0 + HALF],
                    start=True,
                    stop=True,
                )
            cols = slice(first, first + count)
            emptying(h[t][:, cols], acc[:])
            h_banks.append((t, cols, acc))

        def put_h(t, first, count):
            nc.scalar.activation(ds[t][:].indirect(entries(n1_l, first, count)), h[t][:, first : first + count], ACT.Copy)

        def sixteenth_on_scalar(to, acc):
            nc.scalar.activation(to, acc, ACT.Copy, scale=SIXTEENTH)

        def sixteenth_on_vector(to, acc):
            nc.vector.tensor_scalar(to, acc, SIXTEENTH, None, ALU.mult)

        lead_words = deal("lead_words", "lead_words", U32, d_picked[:], slice(0, 1))
        pick_tokens(0, "x_picked")
        lead_plane = deal("lead_plane", "lead_plane", U8, first_plane[:, :H], slice(0, 1))
        first_product(0, lead_words[:, 0, :], lead_plane[:, 0, :], 0, HALF, sixteenth_on_scalar)
        put_h(0, 0, HALF)
        pick_tokens(HALF, "first_bytes")
        first_product(0, lead_words[:, 0, :], lead_plane[:, 0, :], HALF, HALF, sixteenth_on_vector)
        put_h(0, HALF, HALF)
        rest_plane = deal("rest_plane", "rest_plane", U8, first_plane[:, :H], slice(1, PACK))
        next_words = deal("next_words", "lead_words", U32, d_picked[:], slice(1, 2))
        first_product(1, next_words[:, 0, :], rest_plane[:, 0, :], 0, S, sixteenth_on_vector)
        put_h(1, 0, S)
        last_words = deal("last_words", "lead_plane", U32, d_picked[:], slice(2, PACK))
        for t in range(2, PACK):
            first_product(t, last_words[:, t - 2, :], rest_plane[:, t - 1, :], 0, S, sixteenth_on_vector)
        put_h(2, 0, S)

        sl_th = keep.tile([P, PACK], F32, name="sl_th")
        nc.gpsimd.tensor_tensor(sl_th[:], sl_t[:], th_t[:], ALU.mult)
        bias = keep.tile([P, PACK], F32, name="bias")
        nc.gpsimd.tensor_scalar(bias[:], sl_th[:], -1.0, 0.0, ALU.mult, ALU.add)

        hg = keep.tile([P, PACK, S], F32, name="hg")
        for t, cols, acc in h_banks:
            nc.vector.tensor_scalar(hg[:, t, cols], acc[:], gs_t[:, t : t + 1], SIXTEENTH, ALU.mult, ALU.mult)

        cand_bytes = keep.tile([P, C], U8, name="cand_bytes", tag="h2", align_bytes=MX_ALIGN)
        nc.vector.tensor_copy(cand_bytes[:], x_scale_tab[:].indirect(cand_l[:]))
        cand_plane = place_scale_rows("cand_plane", cand_bytes, C, nc.sync)
        n5_l = load_list("n5_l", n5)
        cand_picked = keep.tile([P, C], U32, name="cand_picked", tag="x_scale_tab", align_bytes=MX_ALIGN)
        nc.vector.tensor_copy(cand_picked[:], x_word_tab[:].indirect(cand_l[:]))

        s = [keep.tile([P, S], F32, name=f"s{u}") for u in range(TILES)]
        sg = [keep.tile([P, PAIR, S], F32, name=f"sg{t}", tag=f"h{t + 1}", align_bytes=MX_ALIGN) for t in range(0, PACK, PAIR)]
        z_woven = keep.tile([P, S, PACK], BF16, name="z_woven", align_bytes=MX_ALIGN)

        def fetch_gate(t, j0, width):
            nc.scalar.activation(
                sg[t // PAIR][:, t % PAIR, j0 : j0 + width],
                ds[t][:].indirect(entries(n2_l, j0, width)),
                ACT.Sigmoid,
                bias=bias[:, t : t + 1],
                scale=sl_t[:, t : t + 1],
            )

        def weave_pair(t, j0, width):
            cols, pair = slice(j0, j0 + width), slice(t, t + PAIR)
            nc.vector.tensor_tensor(
                z_woven[:, cols, pair],
                hg[:, pair, cols].rearrange("p t j -> p j t"),
                sg[t // PAIR][:, :, cols].rearrange("p t j -> p j t"),
                ALU.mult,
            )

        fetch_gate(0, 0, S)
        fetch_gate(1, 0, S)
        put_h(3, 0, S)
        weave_pair(0, 0, S)
        fetch_gate(2, 0, S)
        for j0 in range(0, S, HALF):
            fetch_gate(3, j0, HALF)
            weave_pair(2, j0, HALF)
        z_words = keep.tile([P, S], U32, name="z_words", align_bytes=MX_ALIGN)
        z_plane = keep.tile([P, S], U8, name="z_plane", align_bytes=MX_ALIGN)
        for j0 in range(0, S, HALF):
            cols = slice(j0, j0 + HALF)
            nc.vector.quantize_mx(
                z_words[:, cols].bitcast(FP8X4), z_plane[:, cols], z_woven[:, cols, :].rearrange("p j t -> p (j t)")
            )
        for u in range(TILES):
            rows = slice(u * P, (u + 1) * P)
            for j0 in range(0, S, HALF):
                cols = slice(j0, j0 + HALF)
                bank = (u * S + j0) // HALF
                s_acc = psum.tile([P, HALF], F32, name=f"s_acc{bank}", tag=f"bank{bank}")
                nc.tensor.matmul_mx(
                    out=s_acc[:],
                    lhsT=cand_picked[:, rows].bitcast(FP8X4),
                    lhsT_scale=cand_plane[:, rows],
                    rhs=z_words[:, cols].bitcast(FP8X4),
                    rhs_scale=z_plane[:, cols],
                    start=True,
                    stop=True,
                )
                emptying = sixteenth_on_scalar if u == 0 else sixteenth_on_vector
                emptying(s[u][:, cols], s_acc[:])

        pb, rb, dt = {}, {}, {}

        def fetch_pairs(u):
            pa = keep.tile([P, W], F32, name=f"pa{u}")
            pb[u] = keep.tile([P, W], F32, name=f"pb{u}")
            rb[u] = keep.tile([P, W], F32, name=f"rb{u}")
            nc.scalar.activation(pb[u][:], s[u][:].indirect(n4_l[:]), ACT.Copy)
            nc.scalar.activation(pa[:], s[u][:].indirect(n3_l[:]), ACT.Copy)
            nc.vector.tensor_tensor(rb[u][:], pa[:], pb[u][:], ALU.subtract)

        def put_pb(u):
            dt[u] = keep.tile([P, DT_COLS], F32, name=f"dt{u}")
            nc.scalar.activation(dt[u][:].indirect(n3_l[:]), pb[u][:], ACT.Copy)

        def put_rb(u):
            nc.scalar.activation(dt[u][:].indirect(n4_l[:]), rb[u][:], ACT.Copy)

        def finish(u):
            pieces = [(0, S - LAST), (S - LAST, LAST)] if u == TILES - 1 else [(0, S)]
            for j0, width in pieces:
                cols = slice(j0, j0 + width)
                other = keep.tile([P, width], F32, name=f"other{u}_{j0}")
                nc.scalar.activation(other[:], dt[u][:].indirect(entries(n5_l, j0, width)), ACT.Copy)
                result = keep.tile([P, width], F32, name=f"result{u}_{j0}")
                nc.vector.scalar_tensor_tensor(result[:], other[:], 0.5, dt[u][:, cols], ALU.mult, ALU.max)
                nc.sync.dma_start(out[u * P : (u + 1) * P, cols], result[:])

        stages = [(fetch_pairs, 0), (put_rb, 2), (put_pb, 1), (finish, 3)]
        for step in range(TILES + len(stages) - 1):
            for f, lag in stages:
                if 0 <= step - lag < TILES:
                    f(step - lag)
